import numpy as np
import ml_dtypes


def mxq(x, axis, fmt="e4m3"):
    dtype, down = {"e4m3": (ml_dtypes.float8_e4m3fn, 7), "e5m2": (ml_dtypes.float8_e5m2, 14)}[fmt]
    v = np.moveaxis(np.asarray(x, np.float32).astype(ml_dtypes.bfloat16).astype(np.float64), axis, -1)
    blocks = v.reshape(v.shape[:-1] + (-1, 32))
    amax = np.abs(blocks).max(-1, keepdims=True)
    byte = np.maximum(np.where(amax > 0, np.frexp(amax)[1] - 1 + 127, 0) - down, 1)
    scale = np.exp2(byte - 127.0)
    codes = (blocks / scale).astype(np.float32).astype(dtype).astype(np.float64)
    return np.moveaxis((codes * scale).reshape(v.shape), -1, axis)


WIDE = False


def mx_kscale(k):
    if not WIDE:
        return np.ones(k)
    levels = np.array([10, -10, 5, -5, 0])
    if k % 512:
        return np.exp2(np.random.permutation(np.resize(levels, k // 32))).repeat(32)
    a = np.empty((k // 512, 16))
    for p in range(k // 512):
        a[p, :8] = np.random.permutation(np.resize(levels, 8))
        for g in range(8):
            far = levels[np.abs(levels - a[p, g]) >= 10]
            a[p, g + 8] = far[np.random.randint(len(far))]
    return np.exp2(a.ravel()).repeat(32)


def f64(x):
    return np.asarray(x).astype(np.float64)


def planes(y):
    n, m = y.shape
    v = y.astype(np.float32).astype(ml_dtypes.bfloat16).astype(np.float64).reshape(n // 32, 32, m)
    top = np.abs(v).max(1)
    byte = np.clip(np.where(top > 0, np.frexp(top)[1] - 1 + 127 - 7, 1), 1, 254)
    codes = (v * np.exp2(127.0 - byte)[:, None, :]).reshape(n, m).astype(np.float32).astype(ml_dtypes.float8_e4m3fn).view(np.uint8)
    words = codes.reshape(n // 512, 128, 4, m).transpose(0, 1, 3, 2)
    return np.ascontiguousarray(words), np.ascontiguousarray(byte.astype(np.uint8).reshape(n // 512, 16, m))


def split(x):
    m, e = np.frexp(f64(x))
    hi = np.ldexp(np.trunc(16.0 * m) / 16.0, e)
    return hi, f64(x) - hi


K, M, T = 1024, 1536, 512


def setup_inputs():
    n = np.random.standard_normal
    s = mx_kscale(K)[:, None]
    return {
        "w": (n((K, M)) / np.sqrt(K) / s).astype(np.float32),
        "x": (n((K, T)) * s).astype(np.float32),
        "g": (n((512, 1536))).astype(np.float32),
    }


def reference(w, x, g):
    w_hi, w_lo = split(w)
    w_hi_, w_lo_ = mxq(w_hi, 0, "e4m3"), mxq(w_lo, 0, "e4m3")
    x_hi, x_lo = split(x)
    x_hi_, x_lo_ = mxq(x_hi, 0, "e4m3"), mxq(x_lo, 0, "e4m3")
    y = x_hi_.T @ w_hi_ + x_lo_.T @ w_hi_ + x_hi_.T @ w_lo_
    out_0 = f64(g) * y
    return (out_0,) + planes(out_0)

@@ -1,0 +1,206 @@
+from contextlib import ExitStack
+
+import concourse.mybir as mybir
+
+K, M, T = 1024, 1536, 512
+FLOPS = 3 * 2 * K * M * T
+
+F32 = mybir.dt.float32
+BF16 = mybir.dt.bfloat16
+I32 = mybir.dt.int32
+U32 = mybir.dt.uint32
+U8 = mybir.dt.uint8
+FP8X4 = mybir.dt.float8_e4m3fn_x4
+ALU = mybir.AluOpType
+
+P = 128
+PACK = 4
+K_PASS = P * PACK
+PASSES = K // K_PASS
+BANK = 512
+CHUNKS = [256, 512, 512, 256]
+RUN = 2
+PAIR_MASK = -983056
+STAGE_BUFS = 4
+
+
+def tile_mix_split3_tm_pl_mul_kernel(tc, w, x, g, out_0, out_1, out_2):
+    nc = tc.nc
+    starts = [sum(CHUNKS[:c]) for c in range(len(CHUNKS))]
+    last = len(CHUNKS) - 1
+
+    with ExitStack() as ctx:
+        keep = ctx.enter_context(tc.tile_pool(name="keep", bufs=1))
+        psum = ctx.enter_context(tc.psum_pool(name="psum", bufs=1))
+        ctx.enter_context(tc.manual_schedule())
+
+        raw, stage, codes, scales, gain, acc, result, rounded = {}, {}, {}, {}, {}, {}, {}, {}
+        out_scales = keep.tile([P, M], U8, name="out_scales", align_bytes=64)
+
+        def cols(c):
+            return slice(starts[c], starts[c] + CHUNKS[c])
+
+        def width(u):
+            return T if u[0] == "x" else CHUNKS[u[1]]
+
+        def pieces(u):
+            return 2 if u[0] == "x" else 1
+
+        def tag(u):
+            return "%s%d_%d" % u
+
+        def load(u):
+            kind, c, a = u
+            rows = slice(a * K_PASS, (a + 1) * K_PASS)
+            n = width(u) // pieces(u)
+            for h in range(pieces(u)):
+                src = x[rows, h * n : (h + 1) * n] if kind == "x" else w[rows, cols(c)]
+                raw[u, h] = keep.tile([P, PACK * n], F32, name="raw_%s_%d" % (tag(u), h), align_bytes=64)
+                nc.sync.dma_start(
+                    out=raw[u, h][:].rearrange("p (j n) -> p j n", j=PACK),
+                    in_=src.rearrange("(p j) n -> p j n", j=PACK),
+                )
+
+        def load_gain(c):
+            gain[c] = keep.tile([P, PACK, CHUNKS[c]], F32, name="gain%d" % c, align_bytes=64)
+            nc.sync.dma_start(out=gain[c][:], in_=g[:, cols(c)].rearrange("(p j) n -> p j n", j=PACK))
+
+        def walks(u, part):
+            n = PACK * width(u)
+            dst = stage[u][:, part * n : (part + 1) * n]
+            found = []
+            for h in range(pieces(u)):
+                src = raw[u, h][:]
+                if u[0] == "w":
+                    found.append((
+                        src.rearrange("p (j c i) -> p c j i", j=PACK, i=RUN),
+                        src.bitcast(BF16).rearrange("p (j c i e) -> p c j i e", j=PACK, i=RUN, e=2)[:, :, :, :, 1],
+                        dst.rearrange("p (c i j) -> p c j i", i=RUN, j=PACK),
+                    ))
+                else:
+                    m = P // pieces(u)
+                    for s in range(2):
+                        found.append((
+                            src.rearrange("p (j m s i) -> p s m j i", j=PACK, s=2, i=2)[:, s],
+                            src.bitcast(BF16).rearrange("p (j m s i e) -> p s m j i e", j=PACK, s=2, i=2, e=2)[:, s, :, :, :, 1],
+                            dst.rearrange("p (s i m j) -> p s m j i", s=2, i=2, j=PACK)[:, s, h * m : (h + 1) * m],
+                        ))
+            return found
+
+        def upper(u, copy):
+            stage[u] = keep.tile([P, 2 * PACK * T], BF16, name="stage_" + tag(u), tag="stage", bufs=STAGE_BUFS, align_bytes=64)
+            for full, half, dst in walks(u, 0):
+                copy(out=dst, in_=half)
+
+        def mask(u):
+            pairs = stage[u][:, : PACK * width(u)].bitcast(I32)
+            nc.vector.tensor_scalar(out=pairs, in0=pairs, scalar1=PAIR_MASK, scalar2=None, op0=ALU.bitwise_and)
+
+        def subtract(u):
+            for (full, half, hi), (full2, half2, lo) in zip(walks(u, 0), walks(u, 1)):
+                nc.vector.tensor_tensor(out=lo, in0=full, in1=hi, op=ALU.subtract)
+
+        def quantize(u, parts):
+            n = width(u)
+            if u not in codes:
+                codes[u] = keep.tile([P, 2 * n], U32, name="codes_" + tag(u), align_bytes=64)
+                scales[u] = keep.tile([P, 2 * n], U8, name="scales_" + tag(u), align_bytes=64)
+            lo, hi = parts[0] * n, (parts[-1] + 1) * n
+            nc.vector.quantize_mx(
+                out=codes[u][:, lo:hi].bitcast(FP8X4), scales=scales[u][:, lo:hi],
+                in_=stage[u][:, PACK * lo : PACK * hi],
+            )
+
+        def multiply(c, a, products):
+            n = CHUNKS[c]
+            xu, wu = ("x", 0, a), ("w", c, a)
+            for r in range(PACK):
+                for xp, wp in products:
+                    first = (c, r) not in acc
+                    if first:
+                        acc[c, r] = psum.tile([P, BANK], F32, name="acc%d_%d" % (c, r), tag="bank%d" % ((c % 2) * PACK + r))
+                    xs = slice(xp * T + r * P, xp * T + (r + 1) * P)
+                    ws = slice(wp * n, (wp + 1) * n)
+                    nc.tensor.matmul_mx(
+                        out=acc[c, r][:, :n],
+                        lhsT=codes[xu][:, xs].bitcast(FP8X4), lhsT_scale=scales[xu][:, xs],
+                        rhs=codes[wu][:, ws].bitcast(FP8X4), rhs_scale=scales[wu][:, ws],
+                        start=first, stop=(a == PASSES - 1 and (xp, wp) == (0, 1)),
+                    )
+
+        def scale_by_gain(c, rows):
+            n = CHUNKS[c]
+            if c not in result:
+                result[c] = keep.tile([P, PACK * n], F32, name="result%d" % c, align_bytes=64)
+            for r in rows:
+                nc.vector.tensor_tensor(out=result[c][:, r * n : (r + 1) * n], in0=acc[c, r][:, :n], in1=gain[c][:, r, :], op=ALU.mult)
+                nc.sync.dma_start(
+                    out=out_0[:, cols(c)].rearrange("(p j) n -> p j n", j=PACK)[:, r, :],
+                    in_=result[c][:, r * n : (r + 1) * n],
+                )
+
+        def round_result(c, copy):
+            rounded[c] = keep.tile([P, PACK * CHUNKS[c]], BF16, name="rounded%d" % c, align_bytes=64)
+            copy(
+                out=rounded[c][:].rearrange("p (c i j) -> p c j i", i=RUN, j=PACK),
+                in_=result[c][:].rearrange("p (j c i) -> p c j i", j=PACK, i=RUN),
+            )
+
+        def quantize_result(c):
+            words = keep.tile([P, CHUNKS[c]], U32, name="out_words%d" % c, align_bytes=64)
+            nc.vector.quantize_mx(out=words[:].bitcast(FP8X4), scales=out_scales[:, cols(c)], in_=rounded[c][:])
+            nc.sync.dma_start(
+                out=out_1[0].rearrange("p n i -> p (n i)").bitcast(I32)[:, cols(c)],
+                in_=words[:].bitcast(I32),
+            )
+
+        ALL = [(0, 0), (1, 0), (0, 1)]
+        units = [("w", 0, 0), ("w", 0, 1), ("x", 0, 0), ("x", 0, 1)]
+        units.extend(("w", c, a) for c in range(1, len(CHUNKS)) for a in range(PASSES))
+
+        for u in units:
+            load(u)
+            if u[0] == "w" and u[1] >= 1 and u[2] == 0:
+                load_gain(u[1] - 1)
+        load_gain(last)
+
+        upper(units[0], nc.vector.tensor_copy)
+        upper(units[1], nc.scalar.copy)
+        upper(units[2], nc.scalar.copy)
+        mask(units[0])
+        for i, u in enumerate(units):
+            kind, c, a = u
+            final = i == len(units) - 1
+            if i + 3 < len(units):
+                upper(units[i + 3], nc.scalar.copy)
+            subtract(u)
+            if final:
+                quantize(u, [0])
+                multiply(c, a, ALL[:2])
+                scale_by_gain(c - 1, [0])
+                quantize(u, [1])
+                multiply(c, a, ALL[2:])
+                scale_by_gain(c - 1, [1, 2, 3])
+                round_result(c - 1, nc.scalar.copy)
+                continue
+            mask(units[i + 1])
+            quantize(u, [0, 1])
+            if kind == "x":
+                multiply(0, a, ALL)
+            elif c >= 1:
+                multiply(c, a, ALL)
+                if a == 0 and c < last:
+                    scale_by_gain(c - 1, range(PACK))
+                    round_result(c - 1, nc.scalar.copy)
+                if a == 1:
+                    quantize_result(c - 1)
+        scale_by_gain(last, range(PACK))
+        quantize_result(last - 1)
+        round_result(last, nc.vector.tensor_copy)
+        quantize_result(last)
+        for q in range(4):
+            queue = nc.scalar if q % 2 else nc.sync
+            queue.dma_start(
+                out=out_2[0, 4 * q : 4 * q + 4, :].bitcast(I32),
+                in_=out_scales[32 * q : 32 * q + 4, :].bitcast(I32),
+            )

@@ -18,10 +18,12 @@ PACK = 4
 K_PASS = P * PACK
 PASSES = K // K_PASS
 BANK = 512
-CHUNKS = [256, 512, 512, 256]
+CHUNKS = [256, 256, 512, 256, 256]
+EARLY = 2
 RUN = 2
 PAIR_MASK = -983056
-STAGE_BUFS = 4
+AHEAD = 2
+HI, LO = 0, 1
 
 
 def tile_mix_split3_tm_pl_mul_kernel(tc, w, x, g, out_0, out_1, out_2):
@@ -41,103 +43,109 @@ def tile_mix_split3_tm_pl_mul_kernel(tc, w, x, g, out_0, out_1, out_2):
             return slice(starts[c], starts[c] + CHUNKS[c])
 
         def width(u):
-            return T if u[0] == "x" else CHUNKS[u[1]]
+            return T // 2 if u[0] == "x" else CHUNKS[u[1]]
 
-        def pieces(u):
-            return 2 if u[0] == "x" else 1
-
-        def tag(u):
+        def label(u):
             return "%s%d_%d" % u
 
         def load(u):
             kind, c, a = u
+            if kind == "x" and c == 1:
+                raw[u] = raw["x", 0, a]
+                return
             rows = slice(a * K_PASS, (a + 1) * K_PASS)
-            n = width(u) // pieces(u)
-            for h in range(pieces(u)):
-                src = x[rows, h * n : (h + 1) * n] if kind == "x" else w[rows, cols(c)]
-                raw[u, h] = keep.tile([P, PACK * n], F32, name="raw_%s_%d" % (tag(u), h), align_bytes=64)
-                nc.sync.dma_start(
-                    out=raw[u, h][:].rearrange("p (j n) -> p j n", j=PACK),
-                    in_=src.rearrange("(p j) n -> p j n", j=PACK),
-                )
+            src = x[rows, :] if kind == "x" else w[rows, cols(c)]
+            raw[u] = keep.tile([P, PACK * src.shape[1]], F32, name="raw_" + label(u), align_bytes=64)
+            nc.sync.dma_start(
+                out=raw[u][:].rearrange("p (j n) -> p j n", j=PACK),
+                in_=src.rearrange("(p j) n -> p j n", j=PACK),
+            )
 
         def load_gain(c):
             gain[c] = keep.tile([P, PACK, CHUNKS[c]], F32, name="gain%d" % c, align_bytes=64)
             nc.sync.dma_start(out=gain[c][:], in_=g[:, cols(c)].rearrange("(p j) n -> p j n", j=PACK))
 
-        def walks(u, part):
+        def staged(u, part):
             n = PACK * width(u)
-            dst = stage[u][:, part * n : (part + 1) * n]
-            found = []
-            for h in range(pieces(u)):
-                src = raw[u, h][:]
-                if u[0] == "w":
-                    found.append((
-                        src.rearrange("p (j c i) -> p c j i", j=PACK, i=RUN),
-                        src.bitcast(BF16).rearrange("p (j c i e) -> p c j i e", j=PACK, i=RUN, e=2)[:, :, :, :, 1],
-                        dst.rearrange("p (c i j) -> p c j i", i=RUN, j=PACK),
-                    ))
-                else:
-                    m = P // pieces(u)
-                    for s in range(2):
-                        found.append((
-                            src.rearrange("p (j m s i) -> p s m j i", j=PACK, s=2, i=2)[:, s],
-                            src.bitcast(BF16).rearrange("p (j m s i e) -> p s m j i e", j=PACK, s=2, i=2, e=2)[:, s, :, :, :, 1],
-                            dst.rearrange("p (s i m j) -> p s m j i", s=2, i=2, j=PACK)[:, s, h * m : (h + 1) * m],
-                        ))
-            return found
+            return stage[u][:, part * n : (part + 1) * n]
+
+        def walk_raw(u):
+            if u[0] == "w":
+                return raw[u][:].rearrange("p (j c i) -> p c j i", j=PACK, i=RUN)
+            return raw[u][:].rearrange("p (j m s i) -> p s m j i", j=PACK, s=2, i=2)[:, u[1]]
+
+        def walk_upper(u):
+            halves = raw[u][:].bitcast(BF16)
+            if u[0] == "w":
+                return halves.rearrange("p (j c i e) -> p c j i e", j=PACK, i=RUN, e=2)[:, :, :, :, 1]
+            return halves.rearrange("p (j m s i e) -> p s m j i e", j=PACK, s=2, i=2, e=2)[:, u[1], :, :, :, 1]
+
+        def walk_staged(u, part):
+            if u[0] == "w":
+                return staged(u, part).rearrange("p (c i j) -> p c j i", i=RUN, j=PACK)
+            return staged(u, part).rearrange("p (i m j) -> p m j i", i=2, j=PACK)
+
+        def new_stage(u):
+            stage[u] = keep.tile(
+                [P, 2 * PACK * width(u)], BF16, name="stage_" + label(u), tag="stage", bufs=AHEAD + 1, align_bytes=64
+            )
 
         def upper(u, copy):
-            stage[u] = keep.tile([P, 2 * PACK * T], BF16, name="stage_" + tag(u), tag="stage", bufs=STAGE_BUFS, align_bytes=64)
-            for full, half, dst in walks(u, 0):
-                copy(out=dst, in_=half)
+            copy(out=walk_staged(u, HI), in_=walk_upper(u))
 
         def mask(u):
-            pairs = stage[u][:, : PACK * width(u)].bitcast(I32)
+            pairs = staged(u, HI).bitcast(I32)
             nc.vector.tensor_scalar(out=pairs, in0=pairs, scalar1=PAIR_MASK, scalar2=None, op0=ALU.bitwise_and)
 
         def subtract(u):
-            for (full, half, hi), (full2, half2, lo) in zip(walks(u, 0), walks(u, 1)):
-                nc.vector.tensor_tensor(out=lo, in0=full, in1=hi, op=ALU.subtract)
+            nc.vector.tensor_tensor(out=walk_staged(u, LO), in0=walk_raw(u), in1=walk_staged(u, HI), op=ALU.subtract)
 
-        def quantize(u, parts):
+        def quantize(u, part):
             n = width(u)
-            if u not in codes:
-                codes[u] = keep.tile([P, 2 * n], U32, name="codes_" + tag(u), align_bytes=64)
-                scales[u] = keep.tile([P, 2 * n], U8, name="scales_" + tag(u), align_bytes=64)
-            lo, hi = parts[0] * n, (parts[-1] + 1) * n
-            nc.vector.quantize_mx(
-                out=codes[u][:, lo:hi].bitcast(FP8X4), scales=scales[u][:, lo:hi],
-                in_=stage[u][:, PACK * lo : PACK * hi],
-            )
+            codes[u, part] = keep.tile([P, n], U32, name="codes_%s_%d" % (label(u), part), align_bytes=64)
+            scales[u, part] = keep.tile([P, n], U8, name="scales_%s_%d" % (label(u), part), align_bytes=64)
+            nc.vector.quantize_mx(out=codes[u, part][:].bitcast(FP8X4), scales=scales[u, part][:], in_=staged(u, part))
 
-        def multiply(c, a, products):
+        def multiply(c, a, rows, products):
             n = CHUNKS[c]
-            xu, wu = ("x", 0, a), ("w", c, a)
-            for r in range(PACK):
+            for r in rows:
                 for xp, wp in products:
                     first = (c, r) not in acc
                     if first:
                         acc[c, r] = psum.tile([P, BANK], F32, name="acc%d_%d" % (c, r), tag="bank%d" % ((c % 2) * PACK + r))
-                    xs = slice(xp * T + r * P, xp * T + (r + 1) * P)
-                    ws = slice(wp * n, (wp + 1) * n)
+                    xk, wk = (("x", r // 2, a), xp), (("w", c, a), wp)
+                    xs = slice((r % 2) * P, (r % 2 + 1) * P)
                     nc.tensor.matmul_mx(
                         out=acc[c, r][:, :n],
-                        lhsT=codes[xu][:, xs].bitcast(FP8X4), lhsT_scale=scales[xu][:, xs],
-                        rhs=codes[wu][:, ws].bitcast(FP8X4), rhs_scale=scales[wu][:, ws],
-                        start=first, stop=(a == PASSES - 1 and (xp, wp) == (0, 1)),
+                        lhsT=codes[xk][:, xs].bitcast(FP8X4), lhsT_scale=scales[xk][:, xs],
+                        rhs=codes[wk][:].bitcast(FP8X4), rhs_scale=scales[wk][:],
+                        start=first, stop=(a == PASSES - 1 and (xp, wp) == closing[c]),
                     )
+
+        def multiply_ready(u, part):
+            kind, c, a = u
+            if kind == "x":
+                products = [(HI, HI), (HI, LO)] if part == HI else [(LO, HI)]
+                for early in range(EARLY):
+                    multiply(early, a, [2 * c, 2 * c + 1], products)
+            elif c >= EARLY:
+                multiply(c, a, range(PACK), [(HI, HI), (LO, HI)] if part == HI else [(HI, LO)])
+
+        def scale_first_row(c, parked):
+            n = CHUNKS[c]
+            result[c] = keep.tile([P, PACK * n], F32, name="result%d" % c, align_bytes=64)
+            nc.scalar.copy(out=parked, in_=acc[c, 0][:, :n])
+            nc.gpsimd.tensor_tensor(out=result[c][:, :n], in0=parked, in1=gain[c][:, 0, :], op=ALU.mult)
 
         def scale_by_gain(c, rows):
             n = CHUNKS[c]
-            if c not in result:
-                result[c] = keep.tile([P, PACK * n], F32, name="result%d" % c, align_bytes=64)
             for r in rows:
                 nc.vector.tensor_tensor(out=result[c][:, r * n : (r + 1) * n], in0=acc[c, r][:, :n], in1=gain[c][:, r, :], op=ALU.mult)
-                nc.sync.dma_start(
-                    out=out_0[:, cols(c)].rearrange("(p j) n -> p j n", j=PACK)[:, r, :],
-                    in_=result[c][:, r * n : (r + 1) * n],
-                )
+                if r % 2 == 2 - 1:
+                    nc.sync.dma_start(
+                        out=out_0[:, cols(c)].rearrange("(p j) n -> p j n", j=PACK)[:, r + 1 - 2 : r + 1, :],
+                        in_=result[c][:, (r + 1 - 2) * n : (r + 1) * n].rearrange("p (j n) -> p j n", n=n),
+                    )
 
         def round_result(c, copy):
             rounded[c] = keep.tile([P, PACK * CHUNKS[c]], BF16, name="rounded%d" % c, align_bytes=64)
@@ -154,49 +162,55 @@ def tile_mix_split3_tm_pl_mul_kernel(tc, w, x, g, out_0, out_1, out_2):
                 in_=words[:].bitcast(I32),
             )
 
-        ALL = [(0, 0), (1, 0), (0, 1)]
-        units = [("w", 0, 0), ("w", 0, 1), ("x", 0, 0), ("x", 0, 1)]
-        units.extend(("w", c, a) for c in range(1, len(CHUNKS)) for a in range(PASSES))
+        closing = [(LO, HI) if c < EARLY else (HI, LO) for c in range(len(CHUNKS))]
+        units = [("w", c, a) for c in range(EARLY) for a in range(PASSES)]
+        units.extend(("x", s, a) for a in range(PASSES) for s in range(2))
+        late = len(units)
+        units.extend(("w", c, a) for c in range(EARLY, len(CHUNKS)) for a in range(PASSES))
+        final = len(units) - 1
 
-        for u in units:
+        scale_at = {}
+        for c in range(last):
+            done = late - 1 if c < EARLY else units.index(("w", c, PASSES - 1))
+            scale_at[done + (c + 1 if c < EARLY else 2)] = c
+
+        for i, u in enumerate(units):
             load(u)
-            if u[0] == "w" and u[1] >= 1 and u[2] == 0:
-                load_gain(u[1] - 1)
+            if i in scale_at:
+                load_gain(scale_at[i])
         load_gain(last)
 
-        upper(units[0], nc.vector.tensor_copy)
-        upper(units[1], nc.scalar.copy)
-        upper(units[2], nc.scalar.copy)
+        for u in units[:AHEAD]:
+            new_stage(u)
+            upper(u, nc.scalar.copy if u != units[0] else nc.vector.tensor_copy)
         mask(units[0])
         for i, u in enumerate(units):
-            kind, c, a = u
-            final = i == len(units) - 1
-            if i + 3 < len(units):
-                upper(units[i + 3], nc.scalar.copy)
+            if i + AHEAD <= final:
+                coming = units[i + AHEAD]
+                new_stage(coming)
+                if i in scale_at:
+                    scale_first_row(scale_at[i], staged(coming, LO).bitcast(F32)[:, : CHUNKS[scale_at[i]]])
+                upper(coming, nc.scalar.copy)
             subtract(u)
-            if final:
-                quantize(u, [0])
-                multiply(c, a, ALL[:2])
-                scale_by_gain(c - 1, [0])
-                quantize(u, [1])
-                multiply(c, a, ALL[2:])
-                scale_by_gain(c - 1, [1, 2, 3])
-                round_result(c - 1, nc.scalar.copy)
-                continue
-            mask(units[i + 1])
-            quantize(u, [0, 1])
-            if kind == "x":
-                multiply(0, a, ALL)
-            elif c >= 1:
-                multiply(c, a, ALL)
-                if a == 0 and c < last:
-                    scale_by_gain(c - 1, range(PACK))
-                    round_result(c - 1, nc.scalar.copy)
-                if a == 1:
-                    quantize_result(c - 1)
-        scale_by_gain(last, range(PACK))
-        quantize_result(last - 1)
+            if i in scale_at and i < final:
+                scale_by_gain(scale_at[i], [1, 2, 3])
+                round_result(scale_at[i], nc.scalar.copy)
+            quantize(u, HI)
+            multiply_ready(u, HI)
+            if i < final:
+                mask(units[i + 1])
+            if i - 2 in scale_at:
+                quantize_result(scale_at[i - 2])
+            quantize(u, LO)
+            multiply_ready(u, LO)
+        spare = staged(units[final], LO).bitcast(F32)
+        scale_first_row(last - 1, spare[:, : CHUNKS[last - 1]])
+        scale_first_row(last, spare[:, CHUNKS[last - 1] :])
+        scale_by_gain(last - 1, [1, 2, 3])
+        round_result(last - 1, nc.scalar.copy)
+        scale_by_gain(last, [1, 2, 3])
         round_result(last, nc.vector.tensor_copy)
+        quantize_result(last - 1)
         quantize_result(last)
         for q in range(4):
             queue = nc.scalar if q % 2 else nc.sync

@@ -18,12 +18,14 @@ PACK = 4
 K_PASS = P * PACK
 PASSES = K // K_PASS
 BANK = 512
+BANKS = 8
 CHUNKS = [256, 256, 512, 256, 256]
 EARLY = 2
 RUN = 2
 PAIR_MASK = -983056
 AHEAD = 2
 HI, LO = 0, 1
+ROW_ORDER = [0, 2, 3, 1]
 
 
 def tile_mix_split3_tm_pl_mul_kernel(tc, w, x, g, out_0, out_1, out_2):
@@ -37,6 +39,7 @@ def tile_mix_split3_tm_pl_mul_kernel(tc, w, x, g, out_0, out_1, out_2):
         ctx.enter_context(tc.manual_schedule())
 
         raw, stage, codes, scales, gain, acc, result, rounded = {}, {}, {}, {}, {}, {}, {}, {}
+        opened = set()
         out_scales = keep.tile([P, M], U8, name="out_scales", align_bytes=64)
 
         def cols(c):
@@ -62,8 +65,11 @@ def tile_mix_split3_tm_pl_mul_kernel(tc, w, x, g, out_0, out_1, out_2):
             )
 
         def load_gain(c):
-            gain[c] = keep.tile([P, PACK, CHUNKS[c]], F32, name="gain%d" % c, align_bytes=64)
-            nc.sync.dma_start(out=gain[c][:], in_=g[:, cols(c)].rearrange("(p j) n -> p j n", j=PACK))
+            gain[c] = keep.tile([P, PACK * CHUNKS[c]], F32, name="gain%d" % c, align_bytes=64)
+            nc.sync.dma_start(
+                out=gain[c][:].rearrange("p (j n) -> p j n", j=PACK),
+                in_=g[:, cols(c)].rearrange("(p j) n -> p j n", j=PACK),
+            )
 
         def staged(u, part):
             n = PACK * width(u)
@@ -90,68 +96,112 @@ def tile_mix_split3_tm_pl_mul_kernel(tc, w, x, g, out_0, out_1, out_2):
                 [P, 2 * PACK * width(u)], BF16, name="stage_" + label(u), tag="stage", bufs=AHEAD + 1, align_bytes=64
             )
 
-        def upper(u, copy):
-            copy(out=walk_staged(u, HI), in_=walk_upper(u))
+        def share(ap, part, of):
+            n = ap.shape[1] // of
+            return ap[:, part * n : (part + 1) * n]
 
-        def mask(u):
-            pairs = staged(u, HI).bitcast(I32)
+        def upper(u, copy, part=0, of=1):
+            copy(out=share(walk_staged(u, HI), part, of), in_=share(walk_upper(u), part, of))
+
+        def mask(u, part=0, of=1):
+            pairs = share(staged(u, HI).bitcast(I32), part, of)
             nc.vector.tensor_scalar(out=pairs, in0=pairs, scalar1=PAIR_MASK, scalar2=None, op0=ALU.bitwise_and)
 
-        def subtract(u):
-            nc.vector.tensor_tensor(out=walk_staged(u, LO), in0=walk_raw(u), in1=walk_staged(u, HI), op=ALU.subtract)
+        def subtract(u, part=0, of=1):
+            nc.vector.tensor_tensor(
+                out=share(walk_staged(u, LO), part, of), in0=share(walk_raw(u), part, of),
+                in1=share(walk_staged(u, HI), part, of), op=ALU.subtract,
+            )
 
-        def quantize(u, part):
+        def quantize(u, parts):
             n = width(u)
-            codes[u, part] = keep.tile([P, n], U32, name="codes_%s_%d" % (label(u), part), align_bytes=64)
-            scales[u, part] = keep.tile([P, n], U8, name="scales_%s_%d" % (label(u), part), align_bytes=64)
-            nc.vector.quantize_mx(out=codes[u, part][:].bitcast(FP8X4), scales=scales[u, part][:], in_=staged(u, part))
+            name = "%s_%d" % (label(u), parts[0])
+            words = keep.tile([P, n * len(parts)], U32, name="codes_" + name, align_bytes=64)
+            plane = keep.tile([P, n * len(parts)], U8, name="scales_" + name, align_bytes=64)
+            for k, part in enumerate(parts):
+                codes[u, part] = words[:, k * n : (k + 1) * n]
+                scales[u, part] = plane[:, k * n : (k + 1) * n]
+            nc.vector.quantize_mx(
+                out=words[:].bitcast(FP8X4), scales=plane[:],
+                in_=stage[u][:, parts[0] * PACK * n : (parts[-1] + 1) * PACK * n],
+            )
+            multiply_ready(u, parts)
+
+        def rows_per_bank(c):
+            return 2 if CHUNKS[c] < BANK else 1
+
+        def sums(c, rows):
+            n, per = CHUNKS[c], rows_per_bank(c)
+            return acc[c, rows[0] // per][:, (rows[0] % per) * n : (rows[-1] % per + 1) * n]
 
         def multiply(c, a, rows, products):
-            n = CHUNKS[c]
+            per = rows_per_bank(c)
             for r in rows:
                 for xp, wp in products:
-                    first = (c, r) not in acc
+                    first = (c, r // per) not in acc
                     if first:
-                        acc[c, r] = psum.tile([P, BANK], F32, name="acc%d_%d" % (c, r), tag="bank%d" % ((c % 2) * PACK + r))
+                        acc[c, r // per] = psum.tile([P, BANK], F32, name="acc%d_%d" % (c, r), tag="bank", bufs=BANKS)
+                    opened.add((c, r, a, xp, wp))
+                    mates = range(r // per * per, (r // per + 1) * per)
+                    done = sum(1 for k in opened if k[0] == c and k[1] in mates) == 3 * PASSES * per
                     xk, wk = (("x", r // 2, a), xp), (("w", c, a), wp)
                     xs = slice((r % 2) * P, (r % 2 + 1) * P)
                     nc.tensor.matmul_mx(
-                        out=acc[c, r][:, :n],
+                        out=sums(c, [r]),
                         lhsT=codes[xk][:, xs].bitcast(FP8X4), lhsT_scale=scales[xk][:, xs],
-                        rhs=codes[wk][:].bitcast(FP8X4), rhs_scale=scales[wk][:],
-                        start=first, stop=(a == PASSES - 1 and (xp, wp) == closing[c]),
+                        rhs=codes[wk].bitcast(FP8X4), rhs_scale=scales[wk],
+                        start=first, stop=done,
                     )
 
-        def multiply_ready(u, part):
+        def multiply_ready(u, parts):
             kind, c, a = u
             if kind == "x":
-                products = [(HI, HI), (HI, LO)] if part == HI else [(LO, HI)]
+                products = [(xp, wp) for xp, wp in [(HI, HI), (HI, LO), (LO, HI)] if xp in parts]
                 for early in range(EARLY):
                     multiply(early, a, [2 * c, 2 * c + 1], products)
             elif c >= EARLY:
-                multiply(c, a, range(PACK), [(HI, HI), (LO, HI)] if part == HI else [(HI, LO)])
+                products = [(xp, wp) for xp, wp in [(HI, HI), (LO, HI), (HI, LO)] if wp in parts]
+                multiply(c, a, 2==1 and ROW_ORDER or range(PACK), products)
 
-        def scale_first_row(c, parked):
+        def store_rows(c, r):
+            n = CHUNKS[c]
+            nc.sync.dma_start(
+                out=out_0[:, cols(c)].rearrange("(p j) n -> p j n", j=PACK)[:, r : r + 2, :],
+                in_=result[c][:, r * n : (r + 2) * n].rearrange("p (j n) -> p j n", n=n),
+            )
+
+        def scale_rows(c, rows):
+            n, per = CHUNKS[c], rows_per_bank(c)
+            groups = [rows] if per > 1 else [[r] for r in rows]
+            for grp in groups:
+                span = slice(grp[0] * n, (grp[-1] + 1) * n)
+                nc.vector.tensor_tensor(out=result[c][:, span], in0=sums(c, grp), in1=gain[c][:, span], op=ALU.mult)
+
+        def park_first_row(c, parked):
             n = CHUNKS[c]
             result[c] = keep.tile([P, PACK * n], F32, name="result%d" % c, align_bytes=64)
-            nc.scalar.copy(out=parked, in_=acc[c, 0][:, :n])
-            nc.gpsimd.tensor_tensor(out=result[c][:, :n], in0=parked, in1=gain[c][:, 0, :], op=ALU.mult)
+            nc.scalar.copy(out=parked, in_=sums(c, [0]))
+            nc.gpsimd.tensor_tensor(out=result[c][:, :n], in0=parked, in1=gain[c][:, :n], op=ALU.mult)
 
-        def scale_by_gain(c, rows):
-            n = CHUNKS[c]
-            for r in rows:
-                nc.vector.tensor_tensor(out=result[c][:, r * n : (r + 1) * n], in0=acc[c, r][:, :n], in1=gain[c][:, r, :], op=ALU.mult)
-                if r % 2 == 2 - 1:
-                    nc.sync.dma_start(
-                        out=out_0[:, cols(c)].rearrange("(p j) n -> p j n", j=PACK)[:, r + 1 - 2 : r + 1, :],
-                        in_=result[c][:, (r + 1 - 2) * n : (r + 1) * n].rearrange("p (j n) -> p j n", n=n),
-                    )
+        def scale_by_gain(c):
+            if c in result:
+                scale_rows(c, [2, 3])
+                store_rows(c, 2)
+                scale_rows(c, [1])
+                store_rows(c, 0)
+            else:
+                result[c] = keep.tile([P, PACK * CHUNKS[c]], F32, name="result%d" % c, align_bytes=64)
+                for r in (0, 2):
+                    scale_rows(c, [r, r + 1])
+                    store_rows(c, r)
 
-        def round_result(c, copy):
-            rounded[c] = keep.tile([P, PACK * CHUNKS[c]], BF16, name="rounded%d" % c, align_bytes=64)
+        def round_result(c, copy, part, of):
+            if c not in rounded:
+                rounded[c] = keep.tile([P, PACK * CHUNKS[c]], BF16, name="rounded%d" % c, align_bytes=64)
+            n = CHUNKS[c] // RUN // of
             copy(
-                out=rounded[c][:].rearrange("p (c i j) -> p c j i", i=RUN, j=PACK),
-                in_=result[c][:].rearrange("p (j c i) -> p c j i", j=PACK, i=RUN),
+                out=rounded[c][:].rearrange("p (c i j) -> p c j i", i=RUN, j=PACK)[:, part * n : (part + 1) * n],
+                in_=result[c][:].rearrange("p (j c i) -> p c j i", j=PACK, i=RUN)[:, part * n : (part + 1) * n],
             )
 
         def quantize_result(c):
@@ -162,7 +212,6 @@ def tile_mix_split3_tm_pl_mul_kernel(tc, w, x, g, out_0, out_1, out_2):
                 in_=words[:].bitcast(I32),
             )
 
-        closing = [(LO, HI) if c < EARLY else (HI, LO) for c in range(len(CHUNKS))]
         units = [("w", c, a) for c in range(EARLY) for a in range(PASSES)]
         units.extend(("x", s, a) for a in range(PASSES) for s in range(2))
         late = len(units)
@@ -182,35 +231,42 @@ def tile_mix_split3_tm_pl_mul_kernel(tc, w, x, g, out_0, out_1, out_2):
 
         for u in units[:AHEAD]:
             new_stage(u)
-            upper(u, nc.scalar.copy if u != units[0] else nc.vector.tensor_copy)
-        mask(units[0])
-        for i, u in enumerate(units):
+        upper(units[0], nc.vector.tensor_copy, 0, 2)
+        upper(units[0], nc.scalar.copy, 1, 2)
+        upper(units[1], nc.scalar.copy)
+        mask(units[0], 0, 2)
+        mask(units[0], 1, 2)
+        for i, u in enumerate(units[:final]):
             if i + AHEAD <= final:
                 coming = units[i + AHEAD]
                 new_stage(coming)
                 if i in scale_at:
-                    scale_first_row(scale_at[i], staged(coming, LO).bitcast(F32)[:, : CHUNKS[scale_at[i]]])
+                    park_first_row(scale_at[i], staged(coming, LO).bitcast(F32)[:, : CHUNKS[scale_at[i]]])
                 upper(coming, nc.scalar.copy)
-            subtract(u)
-            if i in scale_at and i < final:
-                scale_by_gain(scale_at[i], [1, 2, 3])
-                round_result(scale_at[i], nc.scalar.copy)
-            quantize(u, HI)
-            multiply_ready(u, HI)
-            if i < final:
-                mask(units[i + 1])
+            for part in range(2 if i == 0 else 1):
+                subtract(u, part, 2 if i == 0 else 1)
+            if i in scale_at:
+                scale_by_gain(scale_at[i])
+                round_result(scale_at[i], nc.scalar.copy, 0, 1)
+            apart = i < 1 or i >= late
+            if apart:
+                quantize(u, [HI])
+            mask(units[i + 1])
             if i - 2 in scale_at:
                 quantize_result(scale_at[i - 2])
-            quantize(u, LO)
-            multiply_ready(u, LO)
-        spare = staged(units[final], LO).bitcast(F32)
-        scale_first_row(last - 1, spare[:, : CHUNKS[last - 1]])
-        scale_first_row(last, spare[:, CHUNKS[last - 1] :])
-        scale_by_gain(last - 1, [1, 2, 3])
-        round_result(last - 1, nc.scalar.copy)
-        scale_by_gain(last, [1, 2, 3])
-        round_result(last, nc.vector.tensor_copy)
+            quantize(u, [LO] if apart else [HI, LO])
+        u = units[final]
+        park_first_row(last - 1, staged(units[final - 1], LO).bitcast(F32)[:, : CHUNKS[last - 1]])
+        quantize(u, [HI])
+        subtract(u)
+        scale_by_gain(last - 1)
+        round_result(last - 1, nc.scalar.copy, 0, 1)
+        quantize(u, [LO])
+        quantize_result(last - 2)
+        scale_by_gain(last)
         quantize_result(last - 1)
+        round_result(last, nc.vector.tensor_copy, 0, 2)
+        round_result(last, nc.scalar.copy, 1, 2)
         quantize_result(last)
         for q in range(4):
             queue = nc.scalar if q % 2 else nc.sync

@@ -21,7 +21,7 @@ BANK = 512
 BANKS = 8
 CHUNKS = [256, 256, 512, 256, 256]
 EARLY = 2
-RUN = 2
+RUN = 4
 PAIR_MASK = -983056
 AHEAD = 2
 HI, LO = 0, 1
@@ -233,7 +233,8 @@ def tile_mix_split3_tm_pl_mul_kernel(tc, w, x, g, out_0, out_1, out_2):
             new_stage(u)
         upper(units[0], nc.vector.tensor_copy, 0, 2)
         upper(units[0], nc.scalar.copy, 1, 2)
-        upper(units[1], nc.scalar.copy)
+        upper(units[1], nc.scalar.copy, 0, 2)
+        upper(units[1], nc.scalar.copy, 1, 2)
         mask(units[0], 0, 2)
         mask(units[0], 1, 2)
         for i, u in enumerate(units[:final]):
@@ -243,18 +244,20 @@ def tile_mix_split3_tm_pl_mul_kernel(tc, w, x, g, out_0, out_1, out_2):
                 if i in scale_at:
                     park_first_row(scale_at[i], staged(coming, LO).bitcast(F32)[:, : CHUNKS[scale_at[i]]])
                 upper(coming, nc.scalar.copy)
-            for part in range(2 if i == 0 else 1):
-                subtract(u, part, 2 if i == 0 else 1)
+            for part in range(2 if i <= 1 else 1):
+                subtract(u, part, 2 if i <= 1 else 1)
             if i in scale_at:
                 scale_by_gain(scale_at[i])
                 round_result(scale_at[i], nc.scalar.copy, 0, 1)
             apart = i < 1 or i >= late
             if apart:
                 quantize(u, [HI])
-            mask(units[i + 1])
+            mask(units[i + 1], 0, 2 if i == 0 else 1)
             if i - 2 in scale_at:
                 quantize_result(scale_at[i - 2])
             quantize(u, [LO] if apart else [HI, LO])
+            if i == 0:
+                mask(units[1], 1, 2)
         u = units[final]
         park_first_row(last - 1, staged(units[final - 1], LO).bitcast(F32)[:, : CHUNKS[last - 1]])
         quantize(u, [HI])

from contextlib import ExitStack

import concourse.mybir as mybir

K, M, T = 1024, 1536, 512
FLOPS = 3 * 2 * K * M * T

F32 = mybir.dt.float32
BF16 = mybir.dt.bfloat16
I32 = mybir.dt.int32
U32 = mybir.dt.uint32
U8 = mybir.dt.uint8
FP8X4 = mybir.dt.float8_e4m3fn_x4
ALU = mybir.AluOpType

P = 128
PACK = 4
K_PASS = P * PACK
PASSES = K // K_PASS
BANK = 512
BANKS = 8
CHUNKS = [256, 256, 512, 256, 256]
EARLY = 2
RUN = 4
PAIR_MASK = -983056
AHEAD = 2
HI, LO = 0, 1
ROW_ORDER = [0, 2, 3, 1]


def tile_mix_split3_tm_pl_mul_kernel(tc, w, x, g, out_0, out_1, out_2):
    nc = tc.nc
    starts = [sum(CHUNKS[:c]) for c in range(len(CHUNKS))]
    last = len(CHUNKS) - 1

    with ExitStack() as ctx:
        keep = ctx.enter_context(tc.tile_pool(name="keep", bufs=1))
        psum = ctx.enter_context(tc.psum_pool(name="psum", bufs=1))
        ctx.enter_context(tc.manual_schedule())

        raw, stage, codes, scales, gain, acc, result, rounded = {}, {}, {}, {}, {}, {}, {}, {}
        opened = set()
        out_scales = keep.tile([P, M], U8, name="out_scales", align_bytes=64)

        def cols(c):
            return slice(starts[c], starts[c] + CHUNKS[c])

        def width(u):
            return T // 2 if u[0] == "x" else CHUNKS[u[1]]

        def label(u):
            return "%s%d_%d" % u

        def load(u):
            kind, c, a = u
            if kind == "x" and c == 1:
                raw[u] = raw["x", 0, a]
                return
            rows = slice(a * K_PASS, (a + 1) * K_PASS)
            src = x[rows, :] if kind == "x" else w[rows, cols(c)]
            raw[u] = keep.tile([P, PACK * src.shape[1]], F32, name="raw_" + label(u), align_bytes=64)
            nc.sync.dma_start(
                out=raw[u][:].rearrange("p (j n) -> p j n", j=PACK),
                in_=src.rearrange("(p j) n -> p j n", j=PACK),
            )

        def load_gain(c):
            gain[c] = keep.tile([P, PACK * CHUNKS[c]], F32, name="gain%d" % c, align_bytes=64)
            nc.sync.dma_start(
                out=gain[c][:].rearrange("p (j n) -> p j n", j=PACK),
                in_=g[:, cols(c)].rearrange("(p j) n -> p j n", j=PACK),
            )

        def staged(u, part):
            n = PACK * width(u)
            return stage[u][:, part * n : (part + 1) * n]

        def walk_raw(u):
            if u[0] == "w":
                return raw[u][:].rearrange("p (j c i) -> p c j i", j=PACK, i=RUN)
            return raw[u][:].rearrange("p (j m s i) -> p s m j i", j=PACK, s=2, i=2)[:, u[1]]

        def walk_upper(u):
            halves = raw[u][:].bitcast(BF16)
            if u[0] == "w":
                return halves.rearrange("p (j c i e) -> p c j i e", j=PACK, i=RUN, e=2)[:, :, :, :, 1]
            return halves.rearrange("p (j m s i e) -> p s m j i e", j=PACK, s=2, i=2, e=2)[:, u[1], :, :, :, 1]

        def walk_staged(u, part):
            if u[0] == "w":
                return staged(u, part).rearrange("p (c i j) -> p c j i", i=RUN, j=PACK)
            return staged(u, part).rearrange("p (i m j) -> p m j i", i=2, j=PACK)

        def new_stage(u):
            stage[u] = keep.tile(
                [P, 2 * PACK * width(u)], BF16, name="stage_" + label(u), tag="stage", bufs=AHEAD + 1, align_bytes=64
            )

        def share(ap, part, of):
            n = ap.shape[1] // of
            return ap[:, part * n : (part + 1) * n]

        def upper(u, copy, part=0, of=1):
            copy(out=share(walk_staged(u, HI), part, of), in_=share(walk_upper(u), part, of))

        def mask(u, part=0, of=1):
            pairs = share(staged(u, HI).bitcast(I32), part, of)
            nc.vector.tensor_scalar(out=pairs, in0=pairs, scalar1=PAIR_MASK, scalar2=None, op0=ALU.bitwise_and)

        def subtract(u, part=0, of=1):
            nc.vector.tensor_tensor(
                out=share(walk_staged(u, LO), part, of), in0=share(walk_raw(u), part, of),
                in1=share(walk_staged(u, HI), part, of), op=ALU.subtract,
            )

        def quantize(u, parts):
            n = width(u)
            name = "%s_%d" % (label(u), parts[0])
            words = keep.tile([P, n * len(parts)], U32, name="codes_" + name, align_bytes=64)
            plane = keep.tile([P, n * len(parts)], U8, name="scales_" + name, align_bytes=64)
            for k, part in enumerate(parts):
                codes[u, part] = words[:, k * n : (k + 1) * n]
                scales[u, part] = plane[:, k * n : (k + 1) * n]
            nc.vector.quantize_mx(
                out=words[:].bitcast(FP8X4), scales=plane[:],
                in_=stage[u][:, parts[0] * PACK * n : (parts[-1] + 1) * PACK * n],
            )
            multiply_ready(u, parts)

        def rows_per_bank(c):
            return 2 if CHUNKS[c] < BANK else 1

        def sums(c, rows):
            n, per = CHUNKS[c], rows_per_bank(c)
            return acc[c, rows[0] // per][:, (rows[0] % per) * n : (rows[-1] % per + 1) * n]

        def multiply(c, a, rows, products):
            per = rows_per_bank(c)
            for r in rows:
                for xp, wp in products:
                    first = (c, r // per) not in acc
                    if first:
                        acc[c, r // per] = psum.tile([P, BANK], F32, name="acc%d_%d" % (c, r), tag="bank", bufs=BANKS)
                    opened.add((c, r, a, xp, wp))
                    mates = range(r // per * per, (r // per + 1) * per)
                    done = sum(1 for k in opened if k[0] == c and k[1] in mates) == 3 * PASSES * per
                    xk, wk = (("x", r // 2, a), xp), (("w", c, a), wp)
                    xs = slice((r % 2) * P, (r % 2 + 1) * P)
                    nc.tensor.matmul_mx(
                        out=sums(c, [r]),
                        lhsT=codes[xk][:, xs].bitcast(FP8X4), lhsT_scale=scales[xk][:, xs],
                        rhs=codes[wk].bitcast(FP8X4), rhs_scale=scales[wk],
                        start=first, stop=done,
                    )

        def multiply_ready(u, parts):
            kind, c, a = u
            if kind == "x":
                products = [(xp, wp) for xp, wp in [(HI, HI), (HI, LO), (LO, HI)] if xp in parts]
                for early in range(EARLY):
                    multiply(early, a, [2 * c, 2 * c + 1], products)
            elif c >= EARLY:
                products = [(xp, wp) for xp, wp in [(HI, HI), (LO, HI), (HI, LO)] if wp in parts]
                multiply(c, a, 2==1 and ROW_ORDER or range(PACK), products)

        def store_rows(c, r):
            n = CHUNKS[c]
            nc.sync.dma_start(
                out=out_0[:, cols(c)].rearrange("(p j) n -> p j n", j=PACK)[:, r : r + 2, :],
                in_=result[c][:, r * n : (r + 2) * n].rearrange("p (j n) -> p j n", n=n),
            )

        def scale_rows(c, rows):
            n, per = CHUNKS[c], rows_per_bank(c)
            groups = [rows] if per > 1 else [[r] for r in rows]
            for grp in groups:
                span = slice(grp[0] * n, (grp[-1] + 1) * n)
                nc.vector.tensor_tensor(out=result[c][:, span], in0=sums(c, grp), in1=gain[c][:, span], op=ALU.mult)

        def park_first_row(c, parked):
            n = CHUNKS[c]
            result[c] = keep.tile([P, PACK * n], F32, name="result%d" % c, align_bytes=64)
            nc.scalar.copy(out=parked, in_=sums(c, [0]))
            nc.gpsimd.tensor_tensor(out=result[c][:, :n], in0=parked, in1=gain[c][:, :n], op=ALU.mult)

        def scale_by_gain(c):
            if c in result:
                scale_rows(c, [2, 3])
                store_rows(c, 2)
                scale_rows(c, [1])
                store_rows(c, 0)
            else:
                result[c] = keep.tile([P, PACK * CHUNKS[c]], F32, name="result%d" % c, align_bytes=64)
                for r in (0, 2):
                    scale_rows(c, [r, r + 1])
                    store_rows(c, r)

        def round_result(c, copy, part, of):
            if c not in rounded:
                rounded[c] = keep.tile([P, PACK * CHUNKS[c]], BF16, name="rounded%d" % c, align_bytes=64)
            n = CHUNKS[c] // RUN // of
            copy(
                out=rounded[c][:].rearrange("p (c i j) -> p c j i", i=RUN, j=PACK)[:, part * n : (part + 1) * n],
                in_=result[c][:].rearrange("p (j c i) -> p c j i", j=PACK, i=RUN)[:, part * n : (part + 1) * n],
            )

        def quantize_result(c):
            words = keep.tile([P, CHUNKS[c]], U32, name="out_words%d" % c, align_bytes=64)
            nc.vector.quantize_mx(out=words[:].bitcast(FP8X4), scales=out_scales[:, cols(c)], in_=rounded[c][:])
            nc.sync.dma_start(
                out=out_1[0].rearrange("p n i -> p (n i)").bitcast(I32)[:, cols(c)],
                in_=words[:].bitcast(I32),
            )

        units = [("w", c, a) for c in range(EARLY) for a in range(PASSES)]
        units.extend(("x", s, a) for a in range(PASSES) for s in range(2))
        late = len(units)
        units.extend(("w", c, a) for c in range(EARLY, len(CHUNKS)) for a in range(PASSES))
        final = len(units) - 1

        scale_at = {}
        for c in range(last):
            done = late - 1 if c < EARLY else units.index(("w", c, PASSES - 1))
            scale_at[done + (c + 1 if c < EARLY else 2)] = c

        for i, u in enumerate(units):
            load(u)
            if i in scale_at:
                load_gain(scale_at[i])
        load_gain(last)

        for u in units[:AHEAD]:
            new_stage(u)
        upper(units[0], nc.vector.tensor_copy, 0, 2)
        upper(units[0], nc.scalar.copy, 1, 2)
        upper(units[1], nc.scalar.copy, 0, 2)
        upper(units[1], nc.scalar.copy, 1, 2)
        mask(units[0], 0, 2)
        mask(units[0], 1, 2)
        for i, u in enumerate(units[:final]):
            if i + AHEAD <= final:
                coming = units[i + AHEAD]
                new_stage(coming)
                if i in scale_at:
                    park_first_row(scale_at[i], staged(coming, LO).bitcast(F32)[:, : CHUNKS[scale_at[i]]])
                upper(coming, nc.scalar.copy)
            for part in range(2 if i <= 1 else 1):
                subtract(u, part, 2 if i <= 1 else 1)
            if i in scale_at:
                scale_by_gain(scale_at[i])
                round_result(scale_at[i], nc.scalar.copy, 0, 1)
            apart = i < 1 or i >= late
            if apart:
                quantize(u, [HI])
            mask(units[i + 1], 0, 2 if i == 0 else 1)
            if i - 2 in scale_at:
                quantize_result(scale_at[i - 2])
            quantize(u, [LO] if apart else [HI, LO])
            if i == 0:
                mask(units[1], 1, 2)
        u = units[final]
        park_first_row(last - 1, staged(units[final - 1], LO).bitcast(F32)[:, : CHUNKS[last - 1]])
        quantize(u, [HI])
        subtract(u)
        scale_by_gain(last - 1)
        round_result(last - 1, nc.scalar.copy, 0, 1)
        quantize(u, [LO])
        quantize_result(last - 2)
        scale_by_gain(last)
        quantize_result(last - 1)
        round_result(last, nc.vector.tensor_copy, 0, 2)
        round_result(last, nc.scalar.copy, 1, 2)
        quantize_result(last)
        for q in range(4):
            queue = nc.scalar if q % 2 else nc.sync
            queue.dma_start(
                out=out_2[0, 4 * q : 4 * q + 4, :].bitcast(I32),
                in_=out_scales[32 * q : 32 * q + 4, :].bitcast(I32),
            )
